import numpy as np
import ml_dtypes

BF16 = ml_dtypes.bfloat16


def bf(x):
    return np.asarray(x, np.float32).astype(BF16)


def f32(x):
    return np.asarray(x, np.float32)


def f64(x):
    return np.asarray(x).astype(np.float64)


def striped(idx):
    return np.tile(idx.reshape(-1, 16).T, (8, 1))


S, K, M, N, E, Q = 256, 128, 512, 256, 4, 64


def setup_inputs():
    return {"base": bf(np.random.standard_normal((M, S))), "x": bf(np.random.standard_normal((K, N))), "w": bf(np.random.standard_normal((E, K, M)) / np.sqrt(K)), "b": f32(0.5 * np.random.standard_normal((M, 1))), "offs": striped(np.random.permutation(S))}


def reference(base, x, w, b, offs):
    idx = offs[:16].T.reshape(-1)
    z = f64(base).copy()
    for e in range(E):
        z[:, idx[e * Q : (e + 1) * Q]] += f64(w)[e].T @ f64(x)[:, e * Q : (e + 1) * Q]
    return z + f64(b)

@@ -1,0 +1,68 @@
+import concourse.mybir as mybir
+from concourse.masks import make_identity
+
+BF16, F32, U16 = mybir.dt.bfloat16, mybir.dt.float32, mybir.dt.uint16
+
+P = 128
+TOKENS = 256
+FEATURES = 512
+EXPERTS = 4
+PIECE = 64
+BLOCKS = FEATURES // P
+PIECE_COLS = PIECE // 16
+
+FLOPS = 2 * P * FEATURES * EXPERTS * PIECE
+
+
+def tile_scatter_matmul_kernel(tc, base, x, w, b, offs, out):
+    nc = tc.nc
+    with (
+        tc.tile_pool(name="held", bufs=1) as held,
+        tc.psum_pool(name="windows", bufs=1) as windows,
+    ):
+        offsets = held.tile([P, EXPERTS * PIECE_COLS], U16, name="offsets")
+        nc.sync.dma_start(offsets[:], offs)
+
+        base_sb = held.tile([P, BLOCKS, TOKENS], BF16, name="base_sb")
+        nc.scalar.dma_start(base_sb[:], base.rearrange("(a p) t -> p a t", p=P))
+
+        x_sb = held.tile([P, EXPERTS * PIECE], BF16, name="x_sb")
+        nc.sync.dma_start(x_sb[:], x)
+
+        w_sb = [held.tile([P, FEATURES], BF16, name="w_sb%d" % e) for e in range(EXPERTS)]
+        for e in range(EXPERTS):
+            queue = nc.sync if e % 2 == 0 else nc.scalar
+            queue.dma_start(w_sb[e][:], w[e])
+
+        bias = held.tile([P, BLOCKS], F32, name="bias")
+        with nc.allow_non_contiguous_dma(reason="one float32 to a partition, 512 in all"):
+            nc.gpsimd.dma_start(bias[:], b.rearrange("(a p) o -> p (a o)", p=P))
+
+        ident = held.tile([P, P], BF16, name="ident")
+        make_identity(nc, ident[:])
+
+        window = [windows.tile([P, TOKENS], F32, name="window%d" % a) for a in range(BLOCKS)]
+        for a in range(BLOCKS):
+            nc.tensor.matmul(window[a][:], ident[:], base_sb[:, a, :], start=True, stop=False)
+
+        for a in range(BLOCKS):
+            for e in range(EXPERTS):
+                nc.tensor.matmul(
+                    window[a][:].indirect(offsets[:, e * PIECE_COLS : (e + 1) * PIECE_COLS]),
+                    w_sb[e][:, a * P : (a + 1) * P],
+                    x_sb[:, e * PIECE : (e + 1) * PIECE],
+                    start=False,
+                    stop=(e == EXPERTS - 1),
+                )
+
+            z = held.tile([P, TOKENS], F32, name="z%d" % a)
+            if a % 2 == 0:
+                nc.vector.tensor_scalar(
+                    z[:], window[a][:], bias[:, a : a + 1], None, mybir.AluOpType.add
+                )
+            else:
+                nc.scalar.activation(
+                    z[:], window[a][:], mybir.ActivationFunctionType.Identity,
+                    bias=bias[:, a : a + 1],
+                )
+            nc.sync.dma_start(out[a * P : (a + 1) * P, :], z[:])

@@ -11,6 +11,9 @@ PIECE = 64
 BLOCKS = FEATURES // P
 PIECE_COLS = PIECE // 16
 
+WARM_COLS = 256
+WARM_MATMULS = 4
+
 FLOPS = 2 * P * FEATURES * EXPERTS * PIECE
 
 
@@ -20,33 +23,41 @@ def tile_scatter_matmul_kernel(tc, base, x, w, b, offs, out):
         tc.tile_pool(name="held", bufs=1) as held,
         tc.psum_pool(name="windows", bufs=1) as windows,
     ):
-        offsets = held.tile([P, EXPERTS * PIECE_COLS], U16, name="offsets")
-        nc.sync.dma_start(offsets[:], offs)
-
-        base_sb = held.tile([P, BLOCKS, TOKENS], BF16, name="base_sb")
-        nc.scalar.dma_start(base_sb[:], base.rearrange("(a p) t -> p a t", p=P))
-
-        x_sb = held.tile([P, EXPERTS * PIECE], BF16, name="x_sb")
-        nc.sync.dma_start(x_sb[:], x)
-
-        w_sb = [held.tile([P, FEATURES], BF16, name="w_sb%d" % e) for e in range(EXPERTS)]
-        for e in range(EXPERTS):
-            queue = nc.sync if e % 2 == 0 else nc.scalar
-            queue.dma_start(w_sb[e][:], w[e])
-
-        bias = held.tile([P, BLOCKS], F32, name="bias")
-        with nc.allow_non_contiguous_dma(reason="one float32 to a partition, 512 in all"):
-            nc.gpsimd.dma_start(bias[:], b.rearrange("(a p) o -> p (a o)", p=P))
-
+        zeros = held.tile([P, WARM_COLS], BF16, name="zeros")
+        nc.gpsimd.memset(zeros[:], 0.0)
         ident = held.tile([P, P], BF16, name="ident")
         make_identity(nc, ident[:])
 
+        queues = [nc.sync, nc.scalar]
+
+        offsets = held.tile([P, EXPERTS * PIECE_COLS], U16, name="offsets")
+        nc.sync.dma_start(offsets[:], offs)
+
+        bias = held.tile([P, BLOCKS], F32, name="bias")
+        with nc.allow_non_contiguous_dma(reason="one float32 to a partition, 512 in all"):
+            nc.scalar.dma_start(bias[:], b.rearrange("(a p) o -> p (a o)", p=P))
+
+        base_sb = [held.tile([P, TOKENS], BF16, name="base_sb%d" % a) for a in range(BLOCKS)]
+        for a in range(BLOCKS):
+            queues[a % 2].dma_start(base_sb[a][:], base[a * P : (a + 1) * P, :])
+
+        x_sb = held.tile([P, EXPERTS * PIECE], BF16, name="x_sb")
+        nc.scalar.dma_start(x_sb[:], x)
+
+        w_sb = [held.tile([P, FEATURES], BF16, name="w_sb%d" % e) for e in range(EXPERTS)]
+        for e in range(EXPERTS):
+            queues[e % 2].dma_start(w_sb[e][:], w[e])
+
+        unread = windows.tile([P, WARM_COLS], F32, name="unread")
+        for i in range(WARM_MATMULS):
+            nc.tensor.matmul(unread[:], zeros[:, 0:P], zeros[:], start=True, stop=True)
+
         window = [windows.tile([P, TOKENS], F32, name="window%d" % a) for a in range(BLOCKS)]
         for a in range(BLOCKS):
-            nc.tensor.matmul(window[a][:], ident[:], base_sb[:, a, :], start=True, stop=False)
+            nc.tensor.matmul(window[a][:], ident[:], base_sb[a][:], start=True, stop=False)
 
-        for a in range(BLOCKS):
-            for e in range(EXPERTS):
+        for e in range(EXPERTS):
+            for a in range(BLOCKS):
                 nc.tensor.matmul(
                     window[a][:].indirect(offsets[:, e * PIECE_COLS : (e + 1) * PIECE_COLS]),
                     w_sb[e][:, a * P : (a + 1) * P],
@@ -55,14 +66,16 @@ def tile_scatter_matmul_kernel(tc, base, x, w, b, offs, out):
                     stop=(e == EXPERTS - 1),
                 )
 
+        for a in range(BLOCKS):
             z = held.tile([P, TOKENS], F32, name="z%d" % a)
             if a % 2 == 0:
                 nc.vector.tensor_scalar(
                     z[:], window[a][:], bias[:, a : a + 1], None, mybir.AluOpType.add
                 )
+                nc.sync.dma_start(out[a * P : (a + 1) * P, :], z[:])
             else:
                 nc.scalar.activation(
                     z[:], window[a][:], mybir.ActivationFunctionType.Identity,
                     bias=bias[:, a : a + 1],
                 )
-            nc.sync.dma_start(out[a * P : (a + 1) * P, :], z[:])
+                nc.scalar.dma_start(out[a * P : (a + 1) * P, :], z[:])

@@ -19,6 +19,7 @@ FLOPS = 2 * P * FEATURES * EXPERTS * PIECE
 
 def tile_scatter_matmul_kernel(tc, base, x, w, b, offs, out):
     nc = tc.nc
+    identity_fn = mybir.ActivationFunctionType.Identity
     with (
         tc.tile_pool(name="held", bufs=1) as held,
         tc.psum_pool(name="windows", bufs=1) as windows,
@@ -28,26 +29,24 @@ def tile_scatter_matmul_kernel(tc, base, x, w, b, offs, out):
         ident = held.tile([P, P], BF16, name="ident")
         make_identity(nc, ident[:])
 
-        queues = [nc.sync, nc.scalar]
-
         offsets = held.tile([P, EXPERTS * PIECE_COLS], U16, name="offsets")
         nc.sync.dma_start(offsets[:], offs)
 
-        bias = held.tile([P, BLOCKS], F32, name="bias")
-        with nc.allow_non_contiguous_dma(reason="one float32 to a partition, 512 in all"):
-            nc.scalar.dma_start(bias[:], b.rearrange("(a p) o -> p (a o)", p=P))
-
         base_sb = [held.tile([P, TOKENS], BF16, name="base_sb%d" % a) for a in range(BLOCKS)]
-        for a in range(BLOCKS):
-            queues[a % 2].dma_start(base_sb[a][:], base[a * P : (a + 1) * P, :])
-
         x_sb = held.tile([P, EXPERTS * PIECE], BF16, name="x_sb")
-        nc.scalar.dma_start(x_sb[:], x)
-
         w_sb = [held.tile([P, FEATURES], BF16, name="w_sb%d" % e) for e in range(EXPERTS)]
-        for e in range(EXPERTS):
-            queues[e % 2].dma_start(w_sb[e][:], w[e])
+        bias = held.tile([P, BLOCKS], F32, name="bias")
+        loads = [(base_sb[a], base[a * P : (a + 1) * P, :]) for a in range(BLOCKS)]
+        loads.append((x_sb, x))
+        loads.extend((w_sb[e], w[e]) for e in range(EXPERTS))
+        loads.append((bias, b.rearrange("(a p) o -> p (a o)", p=P)))
+        queues = [nc.scalar, nc.sync]
+        with nc.allow_non_contiguous_dma(reason="the bias: one float32 to a partition"):
+            for i, (tile_sb, source) in enumerate(loads):
+                queues[i % 2].dma_start(tile_sb[:], source)
 
+        unused = held.tile([P, 1], F32, name="unused")
+        nc.scalar.activation(unused[:], zeros[:, 0:1], identity_fn)
         unread = windows.tile([P, WARM_COLS], F32, name="unread")
         for i in range(WARM_MATMULS):
             nc.tensor.matmul(unread[:], zeros[:, 0:P], zeros[:], start=True, stop=True)
@@ -56,17 +55,22 @@ def tile_scatter_matmul_kernel(tc, base, x, w, b, offs, out):
         for a in range(BLOCKS):
             nc.tensor.matmul(window[a][:], ident[:], base_sb[a][:], start=True, stop=False)
 
-        for e in range(EXPERTS):
-            for a in range(BLOCKS):
-                nc.tensor.matmul(
-                    window[a][:].indirect(offsets[:, e * PIECE_COLS : (e + 1) * PIECE_COLS]),
-                    w_sb[e][:, a * P : (a + 1) * P],
-                    x_sb[:, e * PIECE : (e + 1) * PIECE],
-                    start=False,
-                    stop=(e == EXPERTS - 1),
-                )
+        def place(e, a):
+            nc.tensor.matmul(
+                window[a][:].indirect(offsets[:, e * PIECE_COLS : (e + 1) * PIECE_COLS]),
+                w_sb[e][:, a * P : (a + 1) * P],
+                x_sb[:, e * PIECE : (e + 1) * PIECE],
+                start=False,
+                stop=(e == EXPERTS - 1),
+            )
 
+        for e in range(EXPERTS // 2):
+            for a in range(BLOCKS):
+                place(e, a)
         for a in range(BLOCKS):
+            for e in range(EXPERTS // 2, EXPERTS):
+                place(e, a)
+
             z = held.tile([P, TOKENS], F32, name="z%d" % a)
             if a % 2 == 0:
                 nc.vector.tensor_scalar(
@@ -74,8 +78,5 @@ def tile_scatter_matmul_kernel(tc, base, x, w, b, offs, out):
                 )
                 nc.sync.dma_start(out[a * P : (a + 1) * P, :], z[:])
             else:
-                nc.scalar.activation(
-                    z[:], window[a][:], mybir.ActivationFunctionType.Identity,
-                    bias=bias[:, a : a + 1],
-                )
+                nc.scalar.activation(z[:], window[a][:], identity_fn, bias=bias[:, a : a + 1])
                 nc.scalar.dma_start(out[a * P : (a + 1) * P, :], z[:])

@@ -11,9 +11,6 @@ PIECE = 64
 BLOCKS = FEATURES // P
 PIECE_COLS = PIECE // 16
 
-WARM_COLS = 256
-WARM_MATMULS = 4
-
 FLOPS = 2 * P * FEATURES * EXPERTS * PIECE
 
 
@@ -24,7 +21,7 @@ def tile_scatter_matmul_kernel(tc, base, x, w, b, offs, out):
         tc.tile_pool(name="held", bufs=1) as held,
         tc.psum_pool(name="windows", bufs=1) as windows,
     ):
-        zeros = held.tile([P, WARM_COLS], BF16, name="zeros")
+        zeros = held.tile([P, 1], BF16, name="zeros")
         nc.gpsimd.memset(zeros[:], 0.0)
         ident = held.tile([P, P], BF16, name="ident")
         make_identity(nc, ident[:])
@@ -47,9 +44,6 @@ def tile_scatter_matmul_kernel(tc, base, x, w, b, offs, out):
 
         unused = held.tile([P, 1], F32, name="unused")
         nc.scalar.activation(unused[:], zeros[:, 0:1], identity_fn)
-        unread = windows.tile([P, WARM_COLS], F32, name="unread")
-        for i in range(WARM_MATMULS):
-            nc.tensor.matmul(unread[:], zeros[:, 0:P], zeros[:], start=True, stop=True)
 
         window = [windows.tile([P, TOKENS], F32, name="window%d" % a) for a in range(BLOCKS)]
         for a in range(BLOCKS):

@@ -10,6 +10,8 @@ EXPERTS = 4
 PIECE = 64
 BLOCKS = FEATURES // P
 PIECE_COLS = PIECE // 16
+WARM_COLS = 512
+WARM_MATMULS = 3
 
 FLOPS = 2 * P * FEATURES * EXPERTS * PIECE
 
@@ -21,7 +23,7 @@ def tile_scatter_matmul_kernel(tc, base, x, w, b, offs, out):
         tc.tile_pool(name="held", bufs=1) as held,
         tc.psum_pool(name="windows", bufs=1) as windows,
     ):
-        zeros = held.tile([P, 1], BF16, name="zeros")
+        zeros = held.tile([P, P], BF16, name="zeros")
         nc.gpsimd.memset(zeros[:], 0.0)
         ident = held.tile([P, P], BF16, name="ident")
         make_identity(nc, ident[:])
@@ -44,6 +46,10 @@ def tile_scatter_matmul_kernel(tc, base, x, w, b, offs, out):
 
         unused = held.tile([P, 1], F32, name="unused")
         nc.scalar.activation(unused[:], zeros[:, 0:1], identity_fn)
+        spare = windows.tile([P, WARM_COLS // P, P], F32, name="spare")
+        zeros_repeated = zeros[:].unsqueeze(1).to_broadcast([P, WARM_COLS // P, P])
+        for i in range(WARM_MATMULS):
+            nc.tensor.matmul(spare[:], zeros[:], zeros_repeated, start=True, stop=True)
 
         window = [windows.tile([P, TOKENS], F32, name="window%d" % a) for a in range(BLOCKS)]
         for a in range(BLOCKS):

@@ -11,7 +11,7 @@ PIECE = 64
 BLOCKS = FEATURES // P
 PIECE_COLS = PIECE // 16
 WARM_COLS = 512
-WARM_MATMULS = 3
+WARM_MATMULS = 2
 
 FLOPS = 2 * P * FEATURES * EXPERTS * PIECE
 
@@ -23,7 +23,7 @@ def tile_scatter_matmul_kernel(tc, base, x, w, b, offs, out):
         tc.tile_pool(name="held", bufs=1) as held,
         tc.psum_pool(name="windows", bufs=1) as windows,
     ):
-        zeros = held.tile([P, P], BF16, name="zeros")
+        zeros = held.tile([P, 1], BF16, name="zeros")
         nc.gpsimd.memset(zeros[:], 0.0)
         ident = held.tile([P, P], BF16, name="ident")
         make_identity(nc, ident[:])
@@ -46,10 +46,15 @@ def tile_scatter_matmul_kernel(tc, base, x, w, b, offs, out):
 
         unused = held.tile([P, 1], F32, name="unused")
         nc.scalar.activation(unused[:], zeros[:, 0:1], identity_fn)
-        spare = windows.tile([P, WARM_COLS // P, P], F32, name="spare")
-        zeros_repeated = zeros[:].unsqueeze(1).to_broadcast([P, WARM_COLS // P, P])
+        spare = windows.tile([P, WARM_COLS], F32, name="spare")
         for i in range(WARM_MATMULS):
-            nc.tensor.matmul(spare[:], zeros[:], zeros_repeated, start=True, stop=True)
+            nc.tensor.matmul(
+                spare[:],
+                zeros[:, 0:1].to_broadcast([P, P]),
+                zeros[:, 0:1].to_broadcast([P, WARM_COLS]),
+                start=True,
+                stop=True,
+            )
 
         window = [windows.tile([P, TOKENS], F32, name="window%d" % a) for a in range(BLOCKS)]
         for a in range(BLOCKS):

import concourse.mybir as mybir
from concourse.masks import make_identity

BF16, F32, U16 = mybir.dt.bfloat16, mybir.dt.float32, mybir.dt.uint16

P = 128
TOKENS = 256
FEATURES = 512
EXPERTS = 4
PIECE = 64
BLOCKS = FEATURES // P
PIECE_COLS = PIECE // 16
WARM_COLS = 512
WARM_MATMULS = 2

FLOPS = 2 * P * FEATURES * EXPERTS * PIECE


def tile_scatter_matmul_kernel(tc, base, x, w, b, offs, out):
    nc = tc.nc
    identity_fn = mybir.ActivationFunctionType.Identity
    with (
        tc.tile_pool(name="held", bufs=1) as held,
        tc.psum_pool(name="windows", bufs=1) as windows,
    ):
        zeros = held.tile([P, 1], BF16, name="zeros")
        nc.gpsimd.memset(zeros[:], 0.0)
        ident = held.tile([P, P], BF16, name="ident")
        make_identity(nc, ident[:])

        offsets = held.tile([P, EXPERTS * PIECE_COLS], U16, name="offsets")
        nc.sync.dma_start(offsets[:], offs)

        base_sb = [held.tile([P, TOKENS], BF16, name="base_sb%d" % a) for a in range(BLOCKS)]
        x_sb = held.tile([P, EXPERTS * PIECE], BF16, name="x_sb")
        w_sb = [held.tile([P, FEATURES], BF16, name="w_sb%d" % e) for e in range(EXPERTS)]
        bias = held.tile([P, BLOCKS], F32, name="bias")
        loads = [(base_sb[a], base[a * P : (a + 1) * P, :]) for a in range(BLOCKS)]
        loads.append((x_sb, x))
        loads.extend((w_sb[e], w[e]) for e in range(EXPERTS))
        loads.append((bias, b.rearrange("(a p) o -> p (a o)", p=P)))
        queues = [nc.scalar, nc.sync]
        with nc.allow_non_contiguous_dma(reason="the bias: one float32 to a partition"):
            for i, (tile_sb, source) in enumerate(loads):
                queues[i % 2].dma_start(tile_sb[:], source)

        unused = held.tile([P, 1], F32, name="unused")
        nc.scalar.activation(unused[:], zeros[:, 0:1], identity_fn)
        spare = windows.tile([P, WARM_COLS], F32, name="spare")
        for i in range(WARM_MATMULS):
            nc.tensor.matmul(
                spare[:],
                zeros[:, 0:1].to_broadcast([P, P]),
                zeros[:, 0:1].to_broadcast([P, WARM_COLS]),
                start=True,
                stop=True,
            )

        window = [windows.tile([P, TOKENS], F32, name="window%d" % a) for a in range(BLOCKS)]
        for a in range(BLOCKS):
            nc.tensor.matmul(window[a][:], ident[:], base_sb[a][:], start=True, stop=False)

        def place(e, a):
            nc.tensor.matmul(
                window[a][:].indirect(offsets[:, e * PIECE_COLS : (e + 1) * PIECE_COLS]),
                w_sb[e][:, a * P : (a + 1) * P],
                x_sb[:, e * PIECE : (e + 1) * PIECE],
                start=False,
                stop=(e == EXPERTS - 1),
            )

        for e in range(EXPERTS // 2):
            for a in range(BLOCKS):
                place(e, a)
        for a in range(BLOCKS):
            for e in range(EXPERTS // 2, EXPERTS):
                place(e, a)

            z = held.tile([P, TOKENS], F32, name="z%d" % a)
            if a % 2 == 0:
                nc.vector.tensor_scalar(
                    z[:], window[a][:], bias[:, a : a + 1], None, mybir.AluOpType.add
                )
                nc.sync.dma_start(out[a * P : (a + 1) * P, :], z[:])
            else:
                nc.scalar.activation(z[:], window[a][:], identity_fn, bias=bias[:, a : a + 1])
                nc.scalar.dma_start(out[a * P : (a + 1) * P, :], z[:])
